import numpy as np
import ml_dtypes


def mxq(x, axis, fmt="e4m3"):
    dtype, down = {"e4m3": (ml_dtypes.float8_e4m3fn, 7), "e5m2": (ml_dtypes.float8_e5m2, 14)}[fmt]
    v = np.moveaxis(np.asarray(x, np.float32).astype(ml_dtypes.bfloat16).astype(np.float64), axis, -1)
    blocks = v.reshape(v.shape[:-1] + (-1, 32))
    amax = np.abs(blocks).max(-1, keepdims=True)
    byte = np.maximum(np.where(amax > 0, np.frexp(amax)[1] - 1 + 127, 0) - down, 1)
    scale = np.exp2(byte - 127.0)
    codes = (blocks / scale).astype(np.float32).astype(dtype).astype(np.float64)
    return np.moveaxis((codes * scale).reshape(v.shape), -1, axis)


WIDE = False


def mx_kscale(k):
    if not WIDE:
        return np.ones(k)
    levels = np.array([10, -10, 5, -5, 0])
    if k % 512:
        return np.exp2(np.random.permutation(np.resize(levels, k // 32))).repeat(32)
    a = np.empty((k // 512, 16))
    for p in range(k // 512):
        a[p, :8] = np.random.permutation(np.resize(levels, 8))
        for g in range(8):
            far = levels[np.abs(levels - a[p, g]) >= 10]
            a[p, g + 8] = far[np.random.randint(len(far))]
    return np.exp2(a.ravel()).repeat(32)


def f64(x):
    return np.asarray(x).astype(np.float64)


def striped(idx):
    return np.tile(np.asarray(idx).reshape(-1, 16).T, (8, 1)).astype(np.uint16)


def unstriped(offs):
    return offs[:16].T.reshape(-1).astype(np.int64)


E2M1 = np.array([0.0, 0.5, 1.0, 1.5, 2.0, 3.0, 4.0, 6.0, -0.0, -0.5, -1.0, -1.5, -2.0, -3.0, -4.0, -6.0])


def pack_weight(w, fmt):
    k, n = w.shape
    w = f64(np.asarray(w, np.float32).astype(ml_dtypes.bfloat16)).reshape(k // 32, 32, n)
    amax = np.abs(w).max(1)
    if fmt == "e4m3":
        byte = np.frexp(amax)[1] - 1 + 127 - 7
    else:
        mant, ex = np.frexp(amax / 6.0)
        byte = np.where(mant > 0.5, ex, ex - 1) + 127
    byte = np.clip(np.where(amax > 0, byte, 1), 1, 254)
    scaled = (w * np.exp2(127.0 - byte)[:, None, :]).reshape(k, n).astype(np.float32)
    by_word = np.ascontiguousarray(scaled.reshape(k // 512, 128, 4, n).transpose(0, 1, 3, 2))
    if fmt == "e4m3":
        words = by_word.astype(ml_dtypes.float8_e4m3fn).view(np.uint8)
    else:
        c = by_word.astype(ml_dtypes.float4_e2m1fn).view(np.uint8) & 0xF
        words = (c[..., 0::2] | (c[..., 1::2] << 4)).reshape(k // 512, 128, 2 * n)
    return np.ascontiguousarray(words), np.ascontiguousarray(byte.astype(np.uint8).reshape(k // 512, 16, n))


def unpack_weight(words, scales, fmt):
    g, _, n = scales.shape
    words = np.ascontiguousarray(words).reshape(g, 128, n, -1)
    if fmt == "e4m3":
        vals = words.view(ml_dtypes.float8_e4m3fn).astype(np.float64)
    else:
        nib = np.empty((g, 128, n, 4), np.uint8)
        nib[..., 0::2] = words & 0xF
        nib[..., 1::2] = words >> 4
        vals = E2M1[nib]
    vals = vals * np.repeat(np.exp2(scales.astype(np.float64) - 127.0), 8, axis=1)[..., None]
    return vals.transpose(0, 1, 3, 2).reshape(g * 512, n)


def bf(x):
    return np.asarray(x, np.float32).astype(ml_dtypes.bfloat16)


def planes(Y):
    r, m = Y.shape
    b = f64(bf(Y)).reshape(r // 32, 32, m)
    amax = np.abs(b).max(1)
    byte = np.clip(np.where(amax > 0, np.frexp(amax)[1] - 1 + 127 - 7, 1), 1, 254)
    codes = (b * np.exp2(127.0 - byte)[:, None, :]).reshape(r, m).astype(np.float32).astype(ml_dtypes.float8_e4m3fn).view(np.uint8)
    words = codes.reshape(r // 512, 128, 4, m).transpose(0, 1, 3, 2)
    return np.ascontiguousarray(words), np.ascontiguousarray(byte.astype(np.uint8).reshape(r // 512, 16, m))


D, T, I, Q, E, Z = 512, 2048, 512, 256, 512, 1024


def setup_inputs():
    n = np.random.standard_normal
    idx = np.random.permutation(T)[:I]
    idx2 = np.random.permutation(Z)[:I]
    idx3 = np.random.permutation(Z)[:I]
    fd = mx_kscale(D)
    fi = mx_kscale(I)
    ti = np.ones(T)
    ti[idx] = fi
    keysp = pack_weight(n((D, T)) / fd[:, None], "e2m1")
    return {
        "query": (n((D, Q)) * 1.0 / np.sqrt(D) * fd[:, None]).astype(np.float32),
        "query2": (n((D, Q)) * 1.0 / np.sqrt(D) * fd[:, None]).astype(np.float32),
        "keys_words": keysp[0],
        "keys_scales": keysp[1],
        "pages": (n((D, Z)) / fd[:, None]).astype(np.float32),
        "os": (np.random.uniform(0.02, 0.08, (1, I)) * fi).astype(np.float32),
        "vals": (n((E, T)) / ti).astype(np.float32),
        "offs": striped(idx),
        "offs2": striped(idx2),
        "offs3": striped(idx3),
    }


def reference(query, query2, keys_words, keys_scales, pages, os, vals, offs, offs2, offs3):
    idx = unstriped(offs)
    idx2 = unstriped(offs2)
    idx3 = unstriped(offs3)
    keysu = unpack_weight(keys_words, keys_scales, "e2m1")
    queryq = mxq(f64(query), 0, "e4m3")
    a = queryq.T @ keysu
    query2q = mxq(f64(query2), 0, "e4m3")
    pagesq = mxq(f64(pages), 0, "e4m3")
    h0 = query2q.T @ pagesq
    s = np.maximum(a[:, idx], h0[:, idx2]) - h0[:, idx3]
    w = np.maximum(s, 0.0)
    wo1 = w * f64(os)
    wt1 = wo1.T
    vt1 = f64(vals)[:, idx].T
    vt1q = mxq(vt1, 0, "e4m3")
    wt1q = mxq(wt1, 0, "e4m3")
    o = vt1q.T @ wt1q
    words, scales = planes(o)
    return o, words, scales

from contextlib import ExitStack

import concourse.mybir as mybir
from concourse.masks import make_identity

D, T, I, Q, E, Z = 512, 2048, 512, 256, 512, 1024
FLOPS = 2 * D * Q * (T + Z) + 2 * I * E * Q

F32 = mybir.dt.float32
BF16 = mybir.dt.bfloat16
I32 = mybir.dt.int32
U32 = mybir.dt.uint32
U16 = mybir.dt.uint16
U8 = mybir.dt.uint8
FP8X4 = mybir.dt.float8_e4m3fn_x4
FP4X4 = mybir.dt.float4_e2m1fn_x4
ALU = mybir.AluOpType
COPY = mybir.ActivationFunctionType.Copy

P = 128
PACK = 4
BANK = 512
Q_TILES = Q // P
LIST_COLS = I // 16


def tile_attend_largestof3_read_lean_pl_kernel(
    tc, query, query2, keys_words, keys_scales, pages, slot_factor, vals, offs, offs2, offs3, out_0, out_1, out_2
):
    nc = tc.nc
    with ExitStack() as ctx:
        keep = ctx.enter_context(tc.tile_pool(name="keep", bufs=1))
        late = ctx.enter_context(tc.tile_pool(name="late", bufs=1))
        score_psum = ctx.enter_context(tc.psum_pool(name="score_psum", bufs=4))
        val_psum = ctx.enter_context(tc.psum_pool(name="val_psum", bufs=4))

        def sb(shape, dtype, name, tag=None):
            return keep.tile(shape, dtype, name=name, tag=tag or name, align_bytes=64)

        def over_values(shape, dtype, name, r, kib):
            return late.tile(shape, dtype, name=name, align_bytes=64, offset=r * T * 4 + kib * 1024)

        key_scales = sb([P, T], U8, "key_scales")
        nc.gpsimd.memset(key_scales[:].bitcast(I32), 0)
        query_raw = sb([P, PACK, Q], F32, "query_raw")
        nc.sync.dma_start(out=query_raw[:], in_=query.rearrange("(p j) q -> p j q", j=PACK))
        for quad in range(4):
            nc.sync.dma_start(
                out=key_scales[32 * quad : 32 * quad + 4, :].bitcast(I32),
                in_=keys_scales[0, 4 * quad : 4 * quad + 4, :].bitcast(I32),
            )
        key_words = []
        for half in range(2):
            words = sb([P, T], U8, "key_words%d" % half)
            nc.sync.dma_start(out=words[:].bitcast(I32), in_=keys_words[0, :, half * T : (half + 1) * T].bitcast(I32))
            key_words.append(words)
        query2_raw = sb([P, PACK, Q], F32, "query2_raw")
        nc.sync.dma_start(out=query2_raw[:], in_=query2.rearrange("(p j) q -> p j q", j=PACK))
        token_list = sb([P, LIST_COLS], U16, "token_list")
        nc.sync.dma_start(token_list[:], offs)
        pages_raw = []
        for c in range(Z // BANK):
            raw = sb([P, PACK, BANK], F32, "pages_raw%d" % c)
            nc.sync.dma_start(
                out=raw[:], in_=pages.rearrange("(p j) z -> p j z", j=PACK)[:, :, c * BANK : (c + 1) * BANK]
            )
            pages_raw.append(raw)
        page_list = sb([P, LIST_COLS], U16, "page_list")
        nc.sync.dma_start(page_list[:], offs2)
        base_list = sb([P, LIST_COLS], U16, "base_list")
        nc.sync.dma_start(base_list[:], offs3)
        factor = sb([P, PACK], F32, "factor")
        nc.sync.dma_start(out=factor[:], in_=slot_factor.rearrange("o (p j) -> p (o j)", j=PACK))
        vals_raw = []
        for r in range(PACK):
            raw = over_values([P, T], F32, "vals_raw%d" % r, r, 0)
            nc.sync.dma_start(out=raw[:], in_=vals.rearrange("(p j) t -> p j t", j=PACK)[:, r, :])
            vals_raw.append(raw)

        ident = sb([P, P], F32, "ident")
        make_identity(nc, ident[:])

        def interleave(engine, dst, src):
            o = dst.rearrange("p (c i) j -> p c j i", i=4)
            s = src.rearrange("p j (c i) -> p c j i", i=4)
            if engine == "vector":
                nc.vector.tensor_copy(out=o, in_=s)
            else:
                nc.scalar.activation(out=o, in_=s, func=COPY)

        def quantise(grouped, name, codes=None):
            width = grouped.shape[1]
            if codes is None:
                codes = sb([P, width], U32, name + "_codes")
            scales = sb([P, width], U8, name + "_scales")
            nc.vector.quantize_mx(
                out=codes[:].bitcast(FP8X4), scales=scales[:], in_=grouped[:].rearrange("p n j -> p (n j)")
            )
            return codes, scales

        def evacuate(engine, dst, src):
            if engine == "vector":
                nc.vector.tensor_copy(out=dst, in_=src)
            else:
                nc.scalar.activation(out=dst, in_=src, func=COPY)

        q_mx = []
        for h in range(Q_TILES):
            g = sb([P, P, PACK], BF16, "q_grouped%d" % h)
            interleave("vector" if h == 0 else "scalar", g[:], query_raw[:, :, h * P : (h + 1) * P])
            q_mx.append(quantise(g, "q%d" % h))

        a_sb = [sb([P, T], F32, "a%d" % h) for h in range(Q_TILES)]

        def token_scores(h, c, engine):
            bank = score_psum.tile([P, BANK], F32, name="score")
            nc.tensor.matmul_mx(
                out=bank[:],
                lhsT=q_mx[h][0][:].bitcast(FP8X4),
                lhsT_scale=q_mx[h][1][:],
                rhs=key_words[c // 2][:, 2 * BANK * (c % 2) : 2 * BANK * (c % 2 + 1)].bitcast(FP4X4),
                rhs_scale=key_scales[:, BANK * c : BANK * (c + 1)],
                start=True,
                stop=True,
            )
            evacuate(engine, a_sb[h][:, BANK * c : BANK * (c + 1)], bank[:])

        for c in range(T // BANK):
            token_scores(0, c, "vector" if c == 1 else "scalar")
        g2 = sb([P, Q, PACK], BF16, "q2_grouped")
        interleave("vector", g2[:], query2_raw[:])
        for c in range(T // BANK):
            token_scores(1, c, "vector" if c == 1 else "scalar")
        q2_codes, q2_scales = quantise(g2, "q2")

        def gather(engine, dst, window, offsets):
            if engine == "vector":
                nc.vector.tensor_copy(out=dst, in_=window.indirect(offsets))
            else:
                nc.scalar.activation(out=dst, in_=window.indirect(offsets), func=COPY)

        a_listed = []
        for h in range(Q_TILES):
            g = sb([P, I], F32, "a_listed%d" % h)
            gather("scalar", g[:], a_sb[h][:], token_list[:])
            a_listed.append(g)

        h_sb = [sb([P, Z], F32, "h%d" % h) for h in range(Q_TILES)]
        half = BANK // 2
        for c in range(Z // BANK):
            grouped = [sb([P, half, PACK], BF16, "pages_grouped%d_%d" % (c, k)) for k in range(2)]
            for k in range(2):
                interleave("vector", grouped[k][:], pages_raw[c][:, :, k * half : (k + 1) * half])
            page_mx = [quantise(grouped[k], "pages%d_%d" % (c, k)) for k in range(2)]
            banks = [score_psum.tile([P, BANK], F32, name="score") for h in range(Q_TILES)]
            for k in range(2):
                for h in range(Q_TILES):
                    nc.tensor.matmul_mx(
                        out=banks[h][:, k * half : (k + 1) * half],
                        lhsT=q2_codes[:, h * P : (h + 1) * P].bitcast(FP8X4),
                        lhsT_scale=q2_scales[:, h * P : (h + 1) * P],
                        rhs=page_mx[k][0][:].bitcast(FP8X4),
                        rhs_scale=page_mx[k][1][:],
                        start=True,
                        stop=True,
                    )
            for h in range(Q_TILES):
                evacuate(
                    "vector" if (c, h) == (1, 0) else "scalar", h_sb[h][:, BANK * c : BANK * (c + 1)], banks[h][:]
                )

        neg_factor = sb([P, PACK], F32, "neg_factor")
        nc.scalar.activation(out=neg_factor[:], in_=factor[:], func=COPY, scale=-1.0)

        def pages_listed(h):
            listed = sb([P, I], F32, "page_listed%d" % h)
            gather("scalar" if h else "vector", listed[:], h_sb[h][:], page_list[:])
            return listed

        def larger_of(h):
            larger = sb([P, I], F32, "larger%d" % h)
            nc.vector.tensor_tensor(larger[:], a_listed[h][:], page_listed[h][:], ALU.max)
            return larger

        def scores(h):
            neg_score = sb([P, I], F32, "neg_score%d" % h)
            nc.vector.tensor_tensor(neg_score[:], h_sb[h][:].indirect(base_list[:]), larger[h][:], ALU.subtract)
            bank = score_psum.tile([P, PACK, P], F32, name="score")
            for j in range(PACK):
                nc.tensor.transpose(bank[:, j, :], neg_score[:, j::PACK], ident[:])
            return bank

        def weights(h, bank):
            g = sb([P, P, PACK], BF16, "w_grouped%d" % h)
            nc.vector.scalar_tensor_tensor(
                out=g[:],
                in0=bank[:].rearrange("p j q -> p q j"),
                scalar=0.0,
                in1=neg_factor[:].unsqueeze(1).to_broadcast([P, P, PACK]),
                op0=ALU.min,
                op1=ALU.mult,
            )
            nc.vector.quantize_mx(
                out=w_codes[:, h * P : (h + 1) * P].bitcast(FP8X4),
                scales=w_scales[:, h * P : (h + 1) * P],
                in_=g[:].rearrange("p q j -> p (q j)"),
            )

        def turned_values(r):
            listed = sb([P, I], BF16, "vals_listed%d" % r)
            gather("scalar", listed[:], vals_raw[r][:], token_list[:])
            words = listed[:].bitcast(F32)
            bank = val_psum.tile([P, 2, P], F32, name="val_turn")
            for u in range(2):
                nc.tensor.transpose(bank[:, u, :], words[:, u::2], ident[:])
            return bank

        def values(r, bank):
            g = over_values([P, P, PACK], BF16, "v_grouped%d" % r, last if r else 0, 4 + r)
            dst = g[:].rearrange("p e j -> p (e j)").bitcast(F32).rearrange("p (e u) -> p e u", u=2)
            src = bank[:].rearrange("p u e -> p e u")
            if r == 0:
                nc.vector.tensor_copy(out=dst, in_=src)
            else:
                nc.scalar.copy(out=dst, in_=src)
            return quantise(g, "v%d" % r, over_values([P, P], U32, "v0_codes", last, 4) if r == 0 else None)

        last = PACK - 1
        page_listed = [pages_listed(h) for h in range(Q_TILES)]
        larger = [larger_of(h) for h in range(Q_TILES)]
        v_banks = [turned_values(r) for r in range(PACK)]
        score_banks = [scores(h) for h in range(Q_TILES)]
        w_codes = sb([P, Q], U32, "w_codes")
        w_scales = sb([P, Q], U8, "w_scales")
        for h in range(Q_TILES):
            weights(h, score_banks[h])
        v_mx = [values(r, v_banks[r]) for r in range(PACK)]

        out_sb = over_values([P, PACK, Q], F32, "out_sb", last, 0)
        out_rows = out_0.rearrange("(p j) q -> p j q", j=PACK)
        for r in range(PACK):
            bank = score_psum.tile([P, Q], F32, name="score")
            nc.tensor.matmul_mx(
                out=bank[:],
                lhsT=v_mx[r][0][:].bitcast(FP8X4),
                lhsT_scale=v_mx[r][1][:],
                rhs=w_codes[:].bitcast(FP8X4),
                rhs_scale=w_scales[:],
                start=True,
                stop=True,
            )
            evacuate("vector" if r % 2 else "scalar", out_sb[:, r, :], bank[:])
            if r == last - 1:
                nc.sync.dma_start(out=out_rows[:, :last, :], in_=out_sb[:, :last, :])
        nc.scalar.dma_start(out=out_rows[:, last, :], in_=out_sb[:, last, :])
        rounded = [sb([P, P, PACK], BF16, "out_grouped%d" % h) for h in range(Q_TILES)]
        for h in range(Q_TILES):
            interleave("vector", rounded[h][:], out_sb[:, :, h * P : (h + 1) * P])
        out_codes = sb([P, Q], U32, "out_codes")
        out_scales = sb([P, Q], U8, "out_scales")
        for h in range(Q_TILES):
            nc.vector.quantize_mx(
                out=out_codes[:, h * P : (h + 1) * P].bitcast(FP8X4),
                scales=out_scales[:, h * P : (h + 1) * P],
                in_=rounded[h][:].rearrange("p q j -> p (q j)"),
            )
        nc.sync.dma_start(
            out=out_1[0].rearrange("p c r -> p (c r)").bitcast(I32), in_=out_codes[:].bitcast(I32)
        )
        for quad in range(4):
            queue = nc.sync if quad < 2 else nc.scalar
            queue.dma_start(
                out=out_2[0, 4 * quad : 4 * quad + 4, :].bitcast(I32),
                in_=out_scales[32 * quad : 32 * quad + 4, :].bitcast(I32),
            )
